import numpy as np
import ml_dtypes


def mxq(x, axis, fmt="e4m3"):
    dtype, down = {"e4m3": (ml_dtypes.float8_e4m3fn, 7), "e5m2": (ml_dtypes.float8_e5m2, 14)}[fmt]
    v = np.moveaxis(np.asarray(x, np.float32).astype(ml_dtypes.bfloat16).astype(np.float64), axis, -1)
    blocks = v.reshape(v.shape[:-1] + (-1, 32))
    amax = np.abs(blocks).max(-1, keepdims=True)
    byte = np.maximum(np.where(amax > 0, np.frexp(amax)[1] - 1 + 127, 0) - down, 1)
    scale = np.exp2(byte - 127.0)
    codes = (blocks / scale).astype(np.float32).astype(dtype).astype(np.float64)
    return np.moveaxis((codes * scale).reshape(v.shape), -1, axis)


WIDE = False


def mx_kscale(k):
    if not WIDE:
        return np.ones(k)
    levels = np.array([10, -10, 5, -5, 0])
    if k % 512:
        return np.exp2(np.random.permutation(np.resize(levels, k // 32))).repeat(32)
    a = np.empty((k // 512, 16))
    for p in range(k // 512):
        a[p, :8] = np.random.permutation(np.resize(levels, 8))
        for g in range(8):
            far = levels[np.abs(levels - a[p, g]) >= 10]
            a[p, g + 8] = far[np.random.randint(len(far))]
    return np.exp2(a.ravel()).repeat(32)


def f64(x):
    return np.asarray(x).astype(np.float64)


def striped(idx):
    return np.tile(np.asarray(idx).reshape(-1, 16).T, (8, 1)).astype(np.uint16)


def unstriped(offs):
    return offs[:16].T.reshape(-1).astype(np.int64)


B, N, T, D, DV, NQ = 2, 512, 2048, 512, 128, 512
CAP = 2.0


def setup_inputs():
    n = np.random.standard_normal
    seg = T // B
    idx = np.concatenate([b * seg + np.random.permutation(seg)[:N] for b in range(B)])
    s = mx_kscale(D)[:, None]
    u = np.ones(T)
    u[idx] = mx_kscale(B * N)
    r = np.random.uniform(0.5, 2.0, T)
    qidx = idx
    k = n((D, T)) / s
    v = n((DV, T)) / (u * r)
    return {
        "xq": (n((D, T)) * s * (0.60 / np.sqrt(D))).astype(np.float32),
        "kT": k.astype(np.float32),
        "vT": v.astype(np.float32),
        "vs": np.tile(u * r, (128, 1)).astype(np.float32),
        "offs": striped(idx),
        "qoffs": striped(qidx),
    }


def reference(xq, kT, vT, vs, offs, qoffs):
    idx = unstriped(offs)
    k = f64(kT)
    v = f64(vT)
    pick = lambda x: x[:, idx].reshape(x.shape[0], B, N).transpose(1, 0, 2)
    q = f64(xq)[:, unstriped(qoffs)].reshape(D, B, NQ).transpose(1, 0, 2)
    score = mxq(q, 1, "e4m3").transpose(0, 2, 1) @ mxq(pick(k), 1, "e4m3")
    score = CAP * np.tanh(score / CAP)
    m = score.max(-1, keepdims=True)
    p = np.exp(score - m)
    total = p.sum(-1, keepdims=True)
    w = p * pick(f64(vs))[:, :1, :]
    y = mxq(w, 2, "e4m3") @ mxq(pick(v).transpose(0, 2, 1), 1, "e4m3")
    y = y / total
    out = np.zeros((DV, T))
    out[:, unstriped(qoffs)] = y.transpose(2, 0, 1).reshape(-1, B * NQ)
    return out

@@ -1,0 +1,250 @@
+from contextlib import ExitStack
+
+import concourse.mybir as mybir
+from concourse.masks import make_identity
+
+P = 128
+B, N, T, D, DV, NQ = 2, 512, 2048, 512, 128, 512
+SEG = T // B
+PACK = 4
+APART = False
+LOADS = "L k00 k10 M q00 q10 s0 k01 v0 k11 q01 q11 s1 v1"
+PLAN = """cak00 gak00 cak10 gak10 quk0 caq00 gaq00 caq10 gaq10 quq0 ss0
+cak01 gak01 cak11 gak11 quk1 caq01 gaq01 caq11 gaq11 quq1
+sc00 sc01 we00 sc02 we01 sc03 we02 we03 ss1 vv0 pr00 pr01 sc10 sc11 we10 sc12 we11 sc13 we12 vv1 we13 sx00 sx01 st0 pr10 sx10 pr11 sx11 st1"""
+SHARES = {"cak00":[["S",1024]],"cak10":[["S",1024]],"caq00":[["S",1024]],"caq10":[["S",1024]],"cak01":[["S",1024]],"cak11":[["S",1024]],"caq01":[["S",1024]],"caq11":[["S",1024]]}
+FLOPS = 2 * B * NQ * N * (D + DV)
+
+F32 = mybir.dt.float32
+BF16 = mybir.dt.bfloat16
+U32 = mybir.dt.uint32
+U16 = mybir.dt.uint16
+U8 = mybir.dt.uint8
+FP8X4 = mybir.dt.float8_e4m3fn_x4
+ACT = mybir.ActivationFunctionType
+ALU = mybir.AluOpType
+
+
+def tile_attend_x_cluster_cap_kernel(tc, xq, kT, vT, vs, offs, qoffs, out):
+    nc = tc.nc
+    with ExitStack() as ctx:
+        keep = ctx.enter_context(tc.tile_pool(name="keep", bufs=1))
+        raws = ctx.enter_context(tc.tile_pool(name="raws", bufs=8))
+        seqs = ctx.enter_context(tc.tile_pool(name="seqs", bufs=2))
+        work = ctx.enter_context(tc.tile_pool(name="work", bufs=4))
+        ps_s = ctx.enter_context(tc.psum_pool(name="ps_s", bufs=2))
+        ps_p = ctx.enter_context(tc.psum_pool(name="ps_p", bufs=2))
+        ps_y = ctx.enter_context(tc.psum_pool(name="ps_y", bufs=2))
+        ps_t = ctx.enter_context(tc.psum_pool(name="ps_t", bufs=2))
+
+        lists = keep.tile([P, B * N // 16], U16, name="lists")
+        qlists = keep.tile([P, B * NQ // 16], U16, name="qlists")
+        words = {}
+        for name in ("k", "q"):
+            for u in range(2):
+                words[name, u] = keep.tile([P, 2 * T], BF16, name="words_%s%d" % (name, u))
+        v_pool = keep.tile([P, T], F32, name="v_pool")
+        s_pool = keep.tile([P, T], F32, name="s_pool")
+        placed = [keep.tile([P, SEG * (b + 1)], F32, name="placed%d" % b) for b in range(B)]
+        ident = keep.tile([P, P], F32, name="ident")
+        warm = keep.tile([P, 1], F32, name="warm")
+
+        source = {"k": kT.rearrange("(p j) w -> p j w", j=PACK), "q": xq.rearrange("(p j) w -> p j w", j=PACK)}
+        raw = {}
+
+        def load_rows(name, u, b):
+            t = raws.tile([P, 2, SEG], F32, name="raw")
+            nc.sync.dma_start(out=t[:], in_=source[name][:, 2 * u : 2 * u + 2, b * SEG : (b + 1) * SEG])
+            raw[name, u, b] = t
+
+        def load_flat(tile, src, b):
+            nc.sync.dma_start(out=tile[:, b * SEG : (b + 1) * SEG], in_=src[:, b * SEG : (b + 1) * SEG])
+
+        for step in LOADS.split():
+            if step == "L":
+                nc.sync.dma_start(lists[:], offs)
+            elif step == "M":
+                nc.sync.dma_start(qlists[:], qoffs)
+            elif step[0] == "s":
+                load_flat(s_pool, vs, int(step[1]))
+            elif step[0] == "v":
+                load_flat(v_pool, vT, int(step[1]))
+            else:
+                load_rows(step[0], int(step[1]), int(step[2]))
+
+        nc.vector.memset(warm[:], 0.0)
+        nc.scalar.activation(warm[:], warm[:], ACT.Exp)
+        make_identity(nc, ident[:])
+        nc.gpsimd.memset(placed[0][:], 0.0)
+        nc.gpsimd.memset(placed[1][:, SEG : 2 * SEG], 0.0)
+
+        def cast(name, u, b, shares):
+            full = words[name, u][:].rearrange("p (w e) -> p w e", e=2)
+            src = raw[name, u, b][:].rearrange("p e w -> p w e")
+            lo = 0
+            for engine, width in shares:
+                o = full[:, b * SEG + lo : b * SEG + lo + width, :]
+                i = src[:, lo : lo + width, :]
+                if engine == "S":
+                    nc.scalar.activation(o, i, ACT.Copy)
+                else:
+                    nc.vector.tensor_copy(o, i)
+                lo += width
+
+        grouped, codes, scales, apart = {}, {}, {}, {}
+
+        def gather(name, u, b):
+            if u == 0:
+                grouped[name, b] = seqs.tile([P, N * PACK], BF16, name="grouped_" + name, align_bytes=64)
+                if APART:
+                    apart[name, b] = seqs.tile([P, 2, N], U32, name="apart_" + name)
+            window = words[name, u][:, 0 : 2 * SEG * (b + 1)].bitcast(U32)
+            index = lists if name == "k" else qlists
+            dest = grouped[name, b][:].bitcast(U32).rearrange("p (n u) -> p n u", u=2)
+            if APART:
+                nc.vector.tensor_copy(apart[name, b][:, u, :], window.indirect(index[:, b * 32 : (b + 1) * 32]))
+                if u == 1:
+                    nc.scalar.copy(dest, apart[name, b][:].rearrange("p u n -> p n u"))
+                return
+            nc.vector.tensor_copy(dest[:, :, u], window.indirect(index[:, b * 32 : (b + 1) * 32]))
+
+        def quantize(name, b):
+            codes[name, b] = seqs.tile([P, N], U32, name="codes_" + name, align_bytes=64)
+            scales[name, b] = seqs.tile([P, N], U8, name="scales_" + name, align_bytes=64)
+            nc.vector.quantize_mx(
+                out=codes[name, b][:].bitcast(FP8X4), scales=scales[name, b][:], in_=grouped[name, b][:]
+            )
+
+        slot_scale, v_codes, v_scales = {}, {}, {}
+
+        def gather_flat(pool_tile, b, name):
+            g = seqs.tile([P, N], F32, name=name)
+            nc.vector.tensor_copy(g[:], pool_tile[:, 0 : SEG * (b + 1)].indirect(lists[:, b * 32 : (b + 1) * 32]))
+            bank = ps_t.tile([P, PACK, P], F32, name="bank_t")
+            slots = g[:].rearrange("p (s t) -> p t s", t=PACK)
+            for t in range(PACK):
+                nc.tensor.transpose(bank[:, t, :], slots[:, t, :], ident[:])
+            return bank
+
+        def prepare_scales(b):
+            bank = gather_flat(s_pool, b, "s_rows")
+            slot_scale[b] = seqs.tile([P, PACK], F32, name="slot_scale")
+            nc.scalar.activation(slot_scale[b][:], bank[:, :, 0], ACT.Copy)
+
+        def prepare_values(b):
+            bank = gather_flat(v_pool, b, "v_rows")
+            g = seqs.tile([P, DV * PACK], BF16, name="grouped_v", align_bytes=64)
+            nc.scalar.activation(g[:].rearrange("p (e t) -> p e t", t=PACK), bank[:].rearrange("p t e -> p e t"), ACT.Copy)
+            v_codes[b] = seqs.tile([P, DV], U32, name="codes_v", align_bytes=64)
+            v_scales[b] = seqs.tile([P, DV], U8, name="scales_v", align_bytes=64)
+            nc.vector.quantize_mx(out=v_codes[b][:].bitcast(FP8X4), scales=v_scales[b][:], in_=g[:])
+
+        sums, w_codes, w_scales = {}, {}, {}
+
+        thirds = {}
+
+        def score(b, j):
+            bank = ps_s.tile([P, N], F32, name="bank_s")
+            cols = slice(j * P, (j + 1) * P)
+            nc.tensor.matmul_mx(
+                out=bank[:],
+                lhsT=codes["q", b][:, cols].bitcast(FP8X4),
+                lhsT_scale=scales["q", b][:, cols],
+                rhs=codes["k", b][:].bitcast(FP8X4),
+                rhs_scale=scales["k", b][:],
+                start=True,
+                stop=True,
+            )
+            th = work.tile([P, PACK, P], F32, name="th")
+            nc.scalar.activation(th[:], bank[:].rearrange("q (s t) -> q t s", t=PACK), ACT.Tanh, scale=0.5)
+            neg = work.tile([P, PACK, P], F32, name="neg")
+            low = work.tile([P, 1], F32, name="low")
+            nc.vector.tensor_scalar(neg[:], th[:], -2.0, None, ALU.mult, ALU.min, accum_out=low[:])
+            p = work.tile([P, PACK, P], F32, name="p")
+            if j == 0:
+                sums[b] = seqs.tile([P, NQ // P], F32, name="sums")
+            nc.scalar.activation(p[:], th[:], ACT.Exp, bias=low[:], scale=2.0, accum_out=sums[b][:, j : j + 1])
+            thirds[b, j] = p
+
+        def weigh(b, j):
+            p = thirds[b, j]
+            turned = ps_p.tile([P, PACK, P], F32, name="turned")
+            for t in range(PACK):
+                nc.tensor.transpose(turned[:, t, :], p[:, t, :], ident[:])
+            w = work.tile([P, P, PACK], BF16, name="w", align_bytes=64)
+            nc.vector.tensor_tensor(
+                w[:],
+                turned[:].rearrange("s t q -> s q t"),
+                slot_scale[b][:].unsqueeze(1).to_broadcast([P, P, PACK]),
+                ALU.mult,
+            )
+            h = j // 2
+            if j % 2 == 0:
+                w_codes[b, h] = work.tile([P, 2 * P], U32, name="codes_w", align_bytes=64)
+                w_scales[b, h] = work.tile([P, 2 * P], U8, name="scales_w", align_bytes=64)
+            here = slice((j % 2) * P, (j % 2 + 1) * P)
+            nc.vector.quantize_mx(
+                out=w_codes[b, h][:, here].bitcast(FP8X4),
+                scales=w_scales[b, h][:, here],
+                in_=w[:].rearrange("s q t -> s (q t)"),
+            )
+
+        inverse = {}
+
+        ready = {}
+
+        def product(b, h):
+            bank = ps_y.tile([P, 2 * P], F32, name="bank_y")
+            nc.tensor.matmul_mx(
+                out=bank[:],
+                lhsT=v_codes[b][:].bitcast(FP8X4),
+                lhsT_scale=v_scales[b][:],
+                rhs=w_codes[b, h][:].bitcast(FP8X4),
+                rhs_scale=w_scales[b, h][:],
+                start=True,
+                stop=True,
+            )
+            y = work.tile([P, 2 * P], F32, name="y")
+            nc.scalar.activation(y[:], bank[:], ACT.Copy)
+            inv = work.tile([P, 2], F32, name="inv")
+            nc.vector.reciprocal(inv[:], sums[b][:, 2 * h : 2 * h + 2])
+            spread = ps_t.tile([P, 2, P], F32, name="bank_t")
+            for i in range(2):
+                nc.tensor.transpose(spread[:, i, :], inv[:, i : i + 1].to_broadcast([P, P]), ident[:])
+            factor = work.tile([P, 2 * P], F32, name="factor")
+            nc.scalar.activation(factor[:], spread[:].rearrange("p i q -> p (i q)"), ACT.Copy)
+            ready[b, h] = (y, factor)
+
+        def scatter(b, h):
+            y, factor = ready[b, h]
+            first = b * 32 + 16 * h
+            nc.vector.tensor_tensor(placed[b][:].indirect(qlists[:, first : first + 16]), y[:], factor[:], ALU.mult)
+
+        def store(b):
+            nc.sync.dma_start(out=out[:, b * SEG : (b + 1) * SEG], in_=placed[b][:, b * SEG : (b + 1) * SEG])
+
+        for step in PLAN.split():
+            kind, rest = step[:2], step[2:]
+            d = [c if c in "kq" else int(c) for c in rest]
+            if kind == "ca":
+                cast(d[0], d[1], d[2], SHARES[step])
+            elif kind == "ga":
+                gather(d[0], d[1], d[2])
+            elif kind == "qu":
+                quantize(d[0], d[1])
+            elif kind == "ss":
+                prepare_scales(d[0])
+            elif kind == "vv":
+                prepare_values(d[0])
+            elif kind == "sc":
+                score(d[0], d[1])
+            elif kind == "we":
+                weigh(d[0], d[1])
+            elif kind == "pr":
+                product(d[0], d[1])
+            elif kind == "sx":
+                scatter(d[0], d[1])
+            elif kind == "st":
+                store(d[0])
+            else:
+                assert False

@@ -7,17 +7,21 @@ P = 128
 B, N, T, D, DV, NQ = 2, 512, 2048, 512, 128, 512
 SEG = T // B
 PACK = 4
-APART = False
-LOADS = "L k00 k10 M q00 q10 s0 k01 v0 k11 q01 q11 s1 v1"
-PLAN = """cak00 gak00 cak10 gak10 quk0 caq00 gaq00 caq10 gaq10 quq0 ss0
-cak01 gak01 cak11 gak11 quk1 caq01 gaq01 caq11 gaq11 quq1
-sc00 sc01 we00 sc02 we01 sc03 we02 we03 ss1 vv0 pr00 pr01 sc10 sc11 we10 sc12 we11 sc13 we12 vv1 we13 sx00 sx01 st0 pr10 sx10 pr11 sx11 st1"""
-SHARES = {"cak00":[["S",1024]],"cak10":[["S",1024]],"caq00":[["S",1024]],"caq10":[["S",1024]],"cak01":[["S",1024]],"cak11":[["S",1024]],"caq01":[["S",1024]],"caq11":[["S",1024]]}
+LOADS = "q01 k112 M L q11 k012 k10 q00 q10 k00 s0 s1 v1 v0"
+PLAN = """cak01 caq10 cak10 caq00 caq01 gaq01 cak00 gaq00 caq11 cak11 gaq11 gak01 gak00 gaq10 ss0 quq1 ss1 quq0 vg0 gak11 quk1 sc10 gak10 we10 quk0 sc13 we13 vg1 vv0 sc12 vv1 sc11 sc00 we00 sp104 sc01 we12 sc03 we11 sc02 sp004 pr124 we03 pr102 pr034 sx034 sx124 we02 we01 sx102 pr002 sx002 pr023 sx023 st1 st0"""
+SHARES = {"cak01": [["S",512],["V",512]], "caq10": [["S",512],["S",256],["V",256]], "cak10": [["S",512],["S",512]], "caq00": [["V",512],["S",512]], "caq01": [["S",512],["V",512]], "cak00": [["S",512],["V",512]], "caq11": [["V",512],["S",512]], "cak11": [["S",512],["S",256],["V",256]]}
+INTER = {("k", 0): "G", ("k", 1): "V", ("q", 0): "G", ("q", 1): "S"}
+VS = "SS"
+BY_G = ((0, 2), (0, 0),)
+NWORK = 4
+NPS = [3,3,1,1]
+ZERO = "Gk0 Gk1 Gi Vq0 Vq1 Vs Gv Gh Gp1 Gp0"
 FLOPS = 2 * B * NQ * N * (D + DV)
 
 F32 = mybir.dt.float32
 BF16 = mybir.dt.bfloat16
 U32 = mybir.dt.uint32
+I32 = mybir.dt.int32
 U16 = mybir.dt.uint16
 U8 = mybir.dt.uint8
 FP8X4 = mybir.dt.float8_e4m3fn_x4
@@ -29,64 +33,94 @@ def tile_attend_x_cluster_cap_kernel(tc, xq, kT, vT, vs, offs, qoffs, out):
     nc = tc.nc
     with ExitStack() as ctx:
         keep = ctx.enter_context(tc.tile_pool(name="keep", bufs=1))
-        raws = ctx.enter_context(tc.tile_pool(name="raws", bufs=8))
+        raws = ctx.enter_context(tc.tile_pool(name="raws", bufs=1))
         seqs = ctx.enter_context(tc.tile_pool(name="seqs", bufs=2))
-        work = ctx.enter_context(tc.tile_pool(name="work", bufs=4))
-        ps_s = ctx.enter_context(tc.psum_pool(name="ps_s", bufs=2))
-        ps_p = ctx.enter_context(tc.psum_pool(name="ps_p", bufs=2))
-        ps_y = ctx.enter_context(tc.psum_pool(name="ps_y", bufs=2))
-        ps_t = ctx.enter_context(tc.psum_pool(name="ps_t", bufs=2))
+        work = ctx.enter_context(tc.tile_pool(name="work", bufs=NWORK))
+        ps_s = ctx.enter_context(tc.psum_pool(name="ps_s", bufs=NPS[0]))
+        ps_p = ctx.enter_context(tc.psum_pool(name="ps_p", bufs=NPS[1]))
+        ps_y = ctx.enter_context(tc.psum_pool(name="ps_y", bufs=NPS[2]))
+        ps_t = ctx.enter_context(tc.psum_pool(name="ps_t", bufs=NPS[3]))
 
         lists = keep.tile([P, B * N // 16], U16, name="lists")
         qlists = keep.tile([P, B * NQ // 16], U16, name="qlists")
-        words = {}
-        for name in ("k", "q"):
-            for u in range(2):
-                words[name, u] = keep.tile([P, 2 * T], BF16, name="words_%s%d" % (name, u))
-        v_pool = keep.tile([P, T], F32, name="v_pool")
-        s_pool = keep.tile([P, T], F32, name="s_pool")
-        placed = [keep.tile([P, SEG * (b + 1)], F32, name="placed%d" % b) for b in range(B)]
+        words, v_pool, s_pool, placed = {}, {}, {}, {}
+        for b in range(B):
+            wide = (b + 1) * SEG
+            for name in ("k", "q"):
+                for u in range(2):
+                    words[name, u, b] = keep.tile([P, 2 * wide], BF16, name="words_%s%d%d" % (name, u, b))
+            s_pool[b] = keep.tile([P, wide], F32, name="s_pool%d" % b)
+            v_pool[b] = keep.tile([P, wide], BF16 if VS[b] == "S" else F32, name="v_pool%d" % b)
+            placed[b] = keep.tile([P, wide], F32, name="placed%d" % b)
         ident = keep.tile([P, P], F32, name="ident")
+        ident_h = keep.tile([P, P], BF16, name="ident_h")
         warm = keep.tile([P, 1], F32, name="warm")
 
         source = {"k": kT.rearrange("(p j) w -> p j w", j=PACK), "q": xq.rearrange("(p j) w -> p j w", j=PACK)}
         raw = {}
 
-        def load_rows(name, u, b):
-            t = raws.tile([P, 2, SEG], F32, name="raw")
-            nc.sync.dma_start(out=t[:], in_=source[name][:, 2 * u : 2 * u + 2, b * SEG : (b + 1) * SEG])
-            raw[name, u, b] = t
+        def load_rows(name, u, b, lo, hi):
+            piece = raws.tile([P, 2, hi - lo], F32, name="raw_%d" % (hi - lo), bufs=5 if hi - lo == SEG else 4)
+            nc.sync.dma_start(
+                out=piece[:],
+                in_=source[name][:, 2 * u : 2 * u + 2, b * SEG + lo : b * SEG + hi],
+            )
+            raw.setdefault((name, u, b), []).append((lo, hi, piece))
 
-        def load_flat(tile, src, b):
-            nc.sync.dma_start(out=tile[:, b * SEG : (b + 1) * SEG], in_=src[:, b * SEG : (b + 1) * SEG])
-
+        v_raw = {}
         for step in LOADS.split():
             if step == "L":
                 nc.sync.dma_start(lists[:], offs)
             elif step == "M":
                 nc.sync.dma_start(qlists[:], qoffs)
             elif step[0] == "s":
-                load_flat(s_pool, vs, int(step[1]))
+                b = int(step[1])
+                nc.sync.dma_start(out=s_pool[b][:, b * SEG : (b + 1) * SEG], in_=vs[:, b * SEG : (b + 1) * SEG])
             elif step[0] == "v":
-                load_flat(v_pool, vT, int(step[1]))
+                b = int(step[1])
+                if VS[b] == "S":
+                    v_raw[b] = raws.tile([P, SEG], F32, name="v_raw%d" % b)
+                    nc.sync.dma_start(out=v_raw[b][:], in_=vT[:, b * SEG : (b + 1) * SEG])
+                else:
+                    nc.sync.dma_start(out=v_pool[b][:, b * SEG : (b + 1) * SEG], in_=vT[:, b * SEG : (b + 1) * SEG])
             else:
-                load_rows(step[0], int(step[1]), int(step[2]))
+                parts = int(step[3]) if len(step) > 3 else 1
+                for i in range(parts):
+                    load_rows(step[0], int(step[1]), int(step[2]), i * SEG // parts, (i + 1) * SEG // parts)
 
         nc.vector.memset(warm[:], 0.0)
         nc.scalar.activation(warm[:], warm[:], ACT.Exp)
-        make_identity(nc, ident[:])
-        nc.gpsimd.memset(placed[0][:], 0.0)
-        nc.gpsimd.memset(placed[1][:, SEG : 2 * SEG], 0.0)
+        def zero(which):
+            for step in which.split():
+                eng = nc.vector if step[0] == "V" else nc.gpsimd
+                if step[1] in "kq":
+                    eng.memset(words[step[1], int(step[2]), 1][:, 0 : 2 * SEG].bitcast(U32), 0)
+                elif step[1] == "s":
+                    eng.memset(s_pool[1][:, 0:SEG], 0.0)
+                elif step[1] == "v":
+                    eng.memset(v_pool[1][:, 0:SEG], 0.0)
+                elif step[1] == "i":
+                    make_identity(nc, ident[:])
+                elif step[1] == "h":
+                    make_identity(nc, ident_h[:])
+                elif step[1] == "p":
+                    b = int(step[2])
+                    eng.memset(placed[b][:, b * SEG : (b + 1) * SEG], 0.0)
+
+        zero(ZERO)
 
         def cast(name, u, b, shares):
-            full = words[name, u][:].rearrange("p (w e) -> p w e", e=2)
-            src = raw[name, u, b][:].rearrange("p e w -> p w e")
+            full = words[name, u, b][:].rearrange("p (w e) -> p w e", e=2)
             lo = 0
             for engine, width in shares:
                 o = full[:, b * SEG + lo : b * SEG + lo + width, :]
-                i = src[:, lo : lo + width, :]
+                for a, z, piece in raw[name, u, b]:
+                    if a <= lo < z:
+                        i = piece[:].rearrange("p e w -> p w e")[:, lo - a : lo - a + width, :]
                 if engine == "S":
                     nc.scalar.activation(o, i, ACT.Copy)
+                elif engine == "G":
+                    nc.gpsimd.tensor_copy(o, i)
                 else:
                     nc.vector.tensor_copy(o, i)
                 lo += width
@@ -94,19 +128,30 @@ def tile_attend_x_cluster_cap_kernel(tc, xq, kT, vT, vs, offs, qoffs, out):
         grouped, codes, scales, apart = {}, {}, {}, {}
 
         def gather(name, u, b):
+            mode = INTER[name, b]
             if u == 0:
                 grouped[name, b] = seqs.tile([P, N * PACK], BF16, name="grouped_" + name, align_bytes=64)
-                if APART:
-                    apart[name, b] = seqs.tile([P, 2, N], U32, name="apart_" + name)
-            window = words[name, u][:, 0 : 2 * SEG * (b + 1)].bitcast(U32)
+                if mode != "step":
+                    apart[name, b] = seqs.tile([P, 2, N], U32, name="apart_" + name, bufs=1)
+            window = words[name, u, b][:].bitcast(U32)
             index = lists if name == "k" else qlists
             dest = grouped[name, b][:].bitcast(U32).rearrange("p (n u) -> p n u", u=2)
-            if APART:
-                nc.vector.tensor_copy(apart[name, b][:, u, :], window.indirect(index[:, b * 32 : (b + 1) * 32]))
+            picked = window.indirect(index[:, b * 32 : (b + 1) * 32])
+            if mode == "step":
+                nc.vector.tensor_copy(dest[:, :, u], picked)
+            else:
+                nc.vector.tensor_copy(apart[name, b][:, u, :], picked)
                 if u == 1:
-                    nc.scalar.copy(dest, apart[name, b][:].rearrange("p u n -> p n u"))
-                return
-            nc.vector.tensor_copy(dest[:, :, u], window.indirect(index[:, b * 32 : (b + 1) * 32]))
+                    src = apart[name, b][:].rearrange("p u n -> p n u")
+                    if mode == "S":
+                        nc.scalar.copy(dest, src)
+                    elif mode == "V":
+                        nc.vector.tensor_copy(
+                            grouped[name, b][:].bitcast(I32).rearrange("p (n u) -> p n u", u=2),
+                            apart[name, b][:].bitcast(I32).rearrange("p u n -> p n u"),
+                        )
+                    else:
+                        nc.gpsimd.tensor_copy(dest, src)
 
         def quantize(name, b):
             codes[name, b] = seqs.tile([P, N], U32, name="codes_" + name, align_bytes=64)
@@ -115,33 +160,46 @@ def tile_attend_x_cluster_cap_kernel(tc, xq, kT, vT, vs, offs, qoffs, out):
                 out=codes[name, b][:].bitcast(FP8X4), scales=scales[name, b][:], in_=grouped[name, b][:]
             )
 
-        slot_scale, v_codes, v_scales = {}, {}, {}
+        s_rows = {}
+        slot_scale, v_codes, v_scales, v_rows = {}, {}, {}, {}
 
-        def gather_flat(pool_tile, b, name):
-            g = seqs.tile([P, N], F32, name=name)
-            nc.vector.tensor_copy(g[:], pool_tile[:, 0 : SEG * (b + 1)].indirect(lists[:, b * 32 : (b + 1) * 32]))
+        def prepare_scales(b):
+            g = seqs.tile([P, N], F32, name="s_rows")
+            s_rows[b] = g
+            nc.vector.tensor_copy(g[:], s_pool[b][:].indirect(lists[:, b * 32 : (b + 1) * 32]))
+            if len([j for j in range(4) if (b, j) in BY_G]) == 4:
+                return
             bank = ps_t.tile([P, PACK, P], F32, name="bank_t")
             slots = g[:].rearrange("p (s t) -> p t s", t=PACK)
             for t in range(PACK):
                 nc.tensor.transpose(bank[:, t, :], slots[:, t, :], ident[:])
-            return bank
-
-        def prepare_scales(b):
-            bank = gather_flat(s_pool, b, "s_rows")
             slot_scale[b] = seqs.tile([P, PACK], F32, name="slot_scale")
             nc.scalar.activation(slot_scale[b][:], bank[:, :, 0], ACT.Copy)
 
+        def gather_values(b):
+            if VS[b] == "S":
+                nc.scalar.activation(v_pool[b][:, b * SEG : (b + 1) * SEG], v_raw[b][:], ACT.Copy)
+                g = seqs.tile([P, N, 2], BF16, name="v_rows_h")
+                nc.scalar.activation(g[:, :, 0], v_pool[b][:].indirect(lists[:, b * 32 : (b + 1) * 32]), ACT.Copy)
+                v_rows[b] = (g[:, :, 0], BF16, ident_h)
+            else:
+                g = seqs.tile([P, N], F32, name="v_rows")
+                nc.vector.tensor_copy(g[:], v_pool[b][:].indirect(lists[:, b * 32 : (b + 1) * 32]))
+                v_rows[b] = (g[:], F32, ident)
+
         def prepare_values(b):
-            bank = gather_flat(v_pool, b, "v_rows")
+            rows, kind, eye = v_rows[b]
+            bank = ps_t.tile([P, PACK, P], kind, name="bank_t")
+            slots = rows.rearrange("p (s t) -> p t s", t=PACK)
+            for t in range(PACK):
+                nc.tensor.transpose(bank[:, t, :], slots[:, t, :], eye[:])
             g = seqs.tile([P, DV * PACK], BF16, name="grouped_v", align_bytes=64)
             nc.scalar.activation(g[:].rearrange("p (e t) -> p e t", t=PACK), bank[:].rearrange("p t e -> p e t"), ACT.Copy)
             v_codes[b] = seqs.tile([P, DV], U32, name="codes_v", align_bytes=64)
             v_scales[b] = seqs.tile([P, DV], U8, name="scales_v", align_bytes=64)
             nc.vector.quantize_mx(out=v_codes[b][:].bitcast(FP8X4), scales=v_scales[b][:], in_=g[:])
 
-        sums, w_codes, w_scales = {}, {}, {}
-
-        thirds = {}
+        sums, w_codes, w_scales, weights = {}, {}, {}, {}
 
         def score(b, j):
             bank = ps_s.tile([P, N], F32, name="bank_s")
@@ -155,70 +213,97 @@ def tile_attend_x_cluster_cap_kernel(tc, xq, kT, vT, vs, offs, qoffs, out):
                 start=True,
                 stop=True,
             )
-            th = work.tile([P, PACK, P], F32, name="th")
-            nc.scalar.activation(th[:], bank[:].rearrange("q (s t) -> q t s", t=PACK), ACT.Tanh, scale=0.5)
-            neg = work.tile([P, PACK, P], F32, name="neg")
-            low = work.tile([P, 1], F32, name="low")
+            th = work.tile([P, PACK, P], F32, name="th", bufs=4)
+            if (b, j) in BY_G:
+                nc.scalar.activation(th[:].rearrange("q t s -> q (t s)"), bank[:], ACT.Tanh, scale=0.5)
+            else:
+                nc.scalar.activation(th[:], bank[:].rearrange("q (s t) -> q t s", t=PACK), ACT.Tanh, scale=0.5)
+            neg = work.tile([P, PACK, P], F32, name="neg", bufs=2)
+            low = work.tile([P, 1], F32, name="low", bufs=4)
             nc.vector.tensor_scalar(neg[:], th[:], -2.0, None, ALU.mult, ALU.min, accum_out=low[:])
-            p = work.tile([P, PACK, P], F32, name="p")
+            p = work.tile([P, PACK, P], F32, name="p", bufs=4)
             if j == 0:
                 sums[b] = seqs.tile([P, NQ // P], F32, name="sums")
+            if (b, j) in BY_G:
+                nc.scalar.activation(p[:], th[:], ACT.Exp, bias=low[:], scale=2.0, accum_out=sums[b][:, j : j + 1])
+                weights[b, j] = p
+                return
             nc.scalar.activation(p[:], th[:], ACT.Exp, bias=low[:], scale=2.0, accum_out=sums[b][:, j : j + 1])
-            thirds[b, j] = p
+            weights[b, j] = p
 
         def weigh(b, j):
-            p = thirds[b, j]
-            turned = ps_p.tile([P, PACK, P], F32, name="turned")
-            for t in range(PACK):
-                nc.tensor.transpose(turned[:, t, :], p[:, t, :], ident[:])
-            w = work.tile([P, P, PACK], BF16, name="w", align_bytes=64)
-            nc.vector.tensor_tensor(
-                w[:],
-                turned[:].rearrange("s t q -> s q t"),
-                slot_scale[b][:].unsqueeze(1).to_broadcast([P, P, PACK]),
-                ALU.mult,
-            )
-            h = j // 2
-            if j % 2 == 0:
-                w_codes[b, h] = work.tile([P, 2 * P], U32, name="codes_w", align_bytes=64)
-                w_scales[b, h] = work.tile([P, 2 * P], U8, name="scales_w", align_bytes=64)
-            here = slice((j % 2) * P, (j % 2 + 1) * P)
+            p = weights[b, j]
+            if (b, j) in BY_G:
+                weighed = work.tile([P, N], BF16, name="weighed", bufs=3)
+                nc.gpsimd.tensor_tensor(weighed[:], p[:].rearrange("q t s -> q (t s)"), s_rows[b][:], ALU.mult)
+                turned = ps_p.tile([P, PACK, P], BF16, name="turned")
+                slots = weighed[:].rearrange("q (s t) -> q t s", t=PACK)
+                for t in range(PACK):
+                    nc.tensor.transpose(turned[:, t, :], slots[:, t, :], ident_h[:])
+            else:
+                turned = ps_p.tile([P, PACK, P], F32, name="turned")
+                for t in range(PACK):
+                    nc.tensor.transpose(turned[:, t, :], p[:, t, :], ident[:])
+            w = work.tile([P, P, PACK], BF16, name="w", align_bytes=64, bufs=4)
+            if j == 0:
+                w_codes[b] = seqs.tile([P, NQ], U32, name="codes_w", align_bytes=64)
+                w_scales[b] = seqs.tile([P, NQ], U8, name="scales_w", align_bytes=64)
+            if (b, j) in BY_G:
+                nc.scalar.activation(w[:], turned[:].rearrange("s t q -> s q t"), ACT.Copy)
+            else:
+                nc.vector.tensor_tensor(
+                    w[:],
+                    turned[:].rearrange("s t q -> s q t"),
+                    slot_scale[b][:].unsqueeze(1).to_broadcast([P, P, PACK]),
+                    ALU.mult,
+                )
+            here = slice(j * P, (j + 1) * P)
             nc.vector.quantize_mx(
-                out=w_codes[b, h][:, here].bitcast(FP8X4),
-                scales=w_scales[b, h][:, here],
+                out=w_codes[b][:, here].bitcast(FP8X4),
+                scales=w_scales[b][:, here],
                 in_=w[:].rearrange("s q t -> s (q t)"),
             )
 
-        inverse = {}
-
         ready = {}
 
-        def product(b, h):
-            bank = ps_y.tile([P, 2 * P], F32, name="bank_y")
+        def product(b, lo, hi):
+            width = (hi - lo) * P
+            bank = ps_y.tile([P, width], F32, name="bank_y")
             nc.tensor.matmul_mx(
                 out=bank[:],
                 lhsT=v_codes[b][:].bitcast(FP8X4),
                 lhsT_scale=v_scales[b][:],
-                rhs=w_codes[b, h][:].bitcast(FP8X4),
-                rhs_scale=w_scales[b, h][:],
+                rhs=w_codes[b][:, lo * P : hi * P].bitcast(FP8X4),
+                rhs_scale=w_scales[b][:, lo * P : hi * P],
                 start=True,
                 stop=True,
             )
-            y = work.tile([P, 2 * P], F32, name="y")
+            y = work.tile([P, width], F32, name="y", bufs=4)
             nc.scalar.activation(y[:], bank[:], ACT.Copy)
-            inv = work.tile([P, 2], F32, name="inv")
-            nc.vector.reciprocal(inv[:], sums[b][:, 2 * h : 2 * h + 2])
-            spread = ps_t.tile([P, 2, P], F32, name="bank_t")
-            for i in range(2):
-                nc.tensor.transpose(spread[:, i, :], inv[:, i : i + 1].to_broadcast([P, P]), ident[:])
-            factor = work.tile([P, 2 * P], F32, name="factor")
-            nc.scalar.activation(factor[:], spread[:].rearrange("p i q -> p (i q)"), ACT.Copy)
-            ready[b, h] = (y, factor)
+            ready[b, lo] = y
 
-        def scatter(b, h):
-            y, factor = ready[b, h]
-            first = b * 32 + 16 * h
-            nc.vector.tensor_tensor(placed[b][:].indirect(qlists[:, first : first + 16]), y[:], factor[:], ALU.mult)
+        factors = {}
+
+        def spread(b, lo, hi):
+            inv = work.tile([P, hi - lo], F32, name="inv", bufs=2)
+            nc.vector.reciprocal(inv[:], sums[b][:, lo:hi])
+            bank = ps_t.tile([P, hi - lo, P], F32, name="bank_t")
+            for i in range(hi - lo):
+                nc.tensor.transpose(bank[:, i, :], inv[:, i : i + 1].to_broadcast([P, P]), ident[:])
+            factor = work.tile([P, (hi - lo) * P], F32, name="factor", bufs=2)
+            nc.scalar.activation(factor[:], bank[:].rearrange("p i q -> p (i q)"), ACT.Copy)
+            for i in range(hi - lo):
+                factors[b, lo + i] = (factor, i)
+
+        def scatter(b, lo, hi):
+            factor, i = factors[b, lo]
+            first = b * 32 + 8 * lo
+            nc.vector.tensor_tensor(
+                placed[b][:].indirect(qlists[:, first : first + 8 * (hi - lo)]),
+                ready[b, lo][:],
+                factor[:, i * P : (i + hi - lo) * P],
+                ALU.mult,
+            )
 
         def store(b):
             nc.sync.dma_start(out=out[:, b * SEG : (b + 1) * SEG], in_=placed[b][:, b * SEG : (b + 1) * SEG])
@@ -234,6 +319,8 @@ def tile_attend_x_cluster_cap_kernel(tc, xq, kT, vT, vs, offs, qoffs, out):
                 quantize(d[0], d[1])
             elif kind == "ss":
                 prepare_scales(d[0])
+            elif kind == "vg":
+                gather_values(d[0])
             elif kind == "vv":
                 prepare_values(d[0])
             elif kind == "sc":
@@ -241,9 +328,11 @@ def tile_attend_x_cluster_cap_kernel(tc, xq, kT, vT, vs, offs, qoffs, out):
             elif kind == "we":
                 weigh(d[0], d[1])
             elif kind == "pr":
-                product(d[0], d[1])
+                product(d[0], d[1], d[2])
+            elif kind == "sp":
+                spread(d[0], d[1], d[2])
             elif kind == "sx":
-                scatter(d[0], d[1])
+                scatter(d[0], d[1], d[2])
             elif kind == "st":
                 store(d[0])
             else:

@@ -7,15 +7,17 @@ P = 128
 B, N, T, D, DV, NQ = 2, 512, 2048, 512, 128, 512
 SEG = T // B
 PACK = 4
-LOADS = "q01 k112 M L q11 k012 k10 q00 q10 k00 s0 s1 v1 v0"
-PLAN = """cak01 caq10 cak10 caq00 caq01 gaq01 cak00 gaq00 caq11 cak11 gaq11 gak01 gak00 gaq10 ss0 quq1 ss1 quq0 vg0 gak11 quk1 sc10 gak10 we10 quk0 sc13 we13 vg1 vv0 sc12 vv1 sc11 sc00 we00 sp104 sc01 we12 sc03 we11 sc02 sp004 pr124 we03 pr102 pr034 sx034 sx124 we02 we01 sx102 pr002 sx002 pr023 sx023 st1 st0"""
-SHARES = {"cak01": [["S",512],["V",512]], "caq10": [["S",512],["S",256],["V",256]], "cak10": [["S",512],["S",512]], "caq00": [["V",512],["S",512]], "caq01": [["S",512],["V",512]], "cak00": [["S",512],["V",512]], "caq11": [["V",512],["S",512]], "cak11": [["S",512],["S",256],["V",256]]}
-INTER = {("k", 0): "G", ("k", 1): "V", ("q", 0): "G", ("q", 1): "S"}
-VS = "SS"
-BY_G = ((0, 2), (0, 0),)
+LOADS = "M k012 L k112 q112 q01 q10 k00 q00 v1 k102 v0 s1 s0"
+PLAN = """cak00 cak11 cak01 caq11 caq01 gaq01 caq00 gak01 gak00 vg1 cak10 gaq11 caq10 quq1 gak11 gaq00 quk1 sc10 sc11 gaq10 sc12 mx10 gak10 vv1 sc13 quk0 ex10 mx11 quq0 vg0 sc00 sc01 ex11 ex12 ex13 sg ss1 mx00 we10 we11 sc02 sc03 ss0 mx01 qw102 ex00 we12 ex03 ex01 vv0 ex02 sp104 we13 we00 pr102 qw124 we01 we03 sp004 sx102 pr124 qw034 we02 qw002 pr034 sx124 st1 sx034 qw023 pr002 sx002 pr023 sx023 st0"""
+SHARES = {"cak00": [["V",512],["S",512]], "cak11": [["S",512],["S",256],["V",256]], "cak01": [["V",512],["V",512]], "caq11": [["S",512],["S",512]], "caq01": [["S",512],["V",512]], "caq00": [["S",1024]], "cak10": [["S",512],["S",256],["V",256]], "caq10": [["S",512],["S",512]]}
+INTER = {("k", 0): "step", ("k", 1): "step", ("q", 0): "V", ("q", 1): "V"}
+VS = "SV"
+BY_G = ()
+BY_S = ((0, 2),)
+NRAW = 7
 NWORK = 4
 NPS = [3,3,1,1]
-ZERO = "Gk0 Gk1 Gi Vq0 Vq1 Vs Gv Gh Gp1 Gp0"
+ZERO = "Gk0 Gk1 Gi Vq0 Vq1 Gv Gh Gp1 Gp0"
 FLOPS = 2 * B * NQ * N * (D + DV)
 
 F32 = mybir.dt.float32
@@ -43,29 +45,33 @@ def tile_attend_x_cluster_cap_kernel(tc, xq, kT, vT, vs, offs, qoffs, out):
 
         lists = keep.tile([P, B * N // 16], U16, name="lists")
         qlists = keep.tile([P, B * NQ // 16], U16, name="qlists")
-        words, v_pool, s_pool, placed = {}, {}, {}, {}
+        words, v_pool, placed = {}, {}, {}
         for b in range(B):
             wide = (b + 1) * SEG
             for name in ("k", "q"):
                 for u in range(2):
                     words[name, u, b] = keep.tile([P, 2 * wide], BF16, name="words_%s%d%d" % (name, u, b))
-            s_pool[b] = keep.tile([P, wide], F32, name="s_pool%d" % b)
             v_pool[b] = keep.tile([P, wide], BF16 if VS[b] == "S" else F32, name="v_pool%d" % b)
             placed[b] = keep.tile([P, wide], F32, name="placed%d" % b)
+        s_pool = keep.tile([P, T], F32, name="s_pool")
+        s_rows = keep.tile([P, B * N], F32, name="s_rows")
         ident = keep.tile([P, P], F32, name="ident")
         ident_h = keep.tile([P, P], BF16, name="ident_h")
         warm = keep.tile([P, 1], F32, name="warm")
 
         source = {"k": kT.rearrange("(p j) w -> p j w", j=PACK), "q": xq.rearrange("(p j) w -> p j w", j=PACK)}
-        raw = {}
+        raw, raw_tiles = {}, {}
 
         def load_rows(name, u, b, lo, hi):
-            piece = raws.tile([P, 2, hi - lo], F32, name="raw_%d" % (hi - lo), bufs=5 if hi - lo == SEG else 4)
+            if lo == 0:
+                raw[name, u, b] = []
+                raw_tiles[name, u, b] = raws.tile([P, 2 * SEG], F32, name="raw", bufs=NRAW)
+            piece = raw_tiles[name, u, b][:, 2 * lo : 2 * hi].rearrange("p (e w) -> p e w", e=2)
             nc.sync.dma_start(
-                out=piece[:],
+                out=piece,
                 in_=source[name][:, 2 * u : 2 * u + 2, b * SEG + lo : b * SEG + hi],
             )
-            raw.setdefault((name, u, b), []).append((lo, hi, piece))
+            raw[name, u, b].append((lo, hi, piece))
 
         v_raw = {}
         for step in LOADS.split():
@@ -75,7 +81,7 @@ def tile_attend_x_cluster_cap_kernel(tc, xq, kT, vT, vs, offs, qoffs, out):
                 nc.sync.dma_start(qlists[:], qoffs)
             elif step[0] == "s":
                 b = int(step[1])
-                nc.sync.dma_start(out=s_pool[b][:, b * SEG : (b + 1) * SEG], in_=vs[:, b * SEG : (b + 1) * SEG])
+                nc.sync.dma_start(out=s_pool[:, b * SEG : (b + 1) * SEG], in_=vs[:, b * SEG : (b + 1) * SEG])
             elif step[0] == "v":
                 b = int(step[1])
                 if VS[b] == "S":
@@ -95,8 +101,6 @@ def tile_attend_x_cluster_cap_kernel(tc, xq, kT, vT, vs, offs, qoffs, out):
                 eng = nc.vector if step[0] == "V" else nc.gpsimd
                 if step[1] in "kq":
                     eng.memset(words[step[1], int(step[2]), 1][:, 0 : 2 * SEG].bitcast(U32), 0)
-                elif step[1] == "s":
-                    eng.memset(s_pool[1][:, 0:SEG], 0.0)
                 elif step[1] == "v":
                     eng.memset(v_pool[1][:, 0:SEG], 0.0)
                 elif step[1] == "i":
@@ -116,7 +120,7 @@ def tile_attend_x_cluster_cap_kernel(tc, xq, kT, vT, vs, offs, qoffs, out):
                 o = full[:, b * SEG + lo : b * SEG + lo + width, :]
                 for a, z, piece in raw[name, u, b]:
                     if a <= lo < z:
-                        i = piece[:].rearrange("p e w -> p w e")[:, lo - a : lo - a + width, :]
+                        i = piece.rearrange("p e w -> p w e")[:, lo - a : lo - a + width, :]
                 if engine == "S":
                     nc.scalar.activation(o, i, ACT.Copy)
                 elif engine == "G":
@@ -160,17 +164,14 @@ def tile_attend_x_cluster_cap_kernel(tc, xq, kT, vT, vs, offs, qoffs, out):
                 out=codes[name, b][:].bitcast(FP8X4), scales=scales[name, b][:], in_=grouped[name, b][:]
             )
 
-        s_rows = {}
         slot_scale, v_codes, v_scales, v_rows = {}, {}, {}, {}
 
+        def gather_scales():
+            nc.vector.tensor_copy(s_rows[:], s_pool[:].indirect(lists[:]))
+
         def prepare_scales(b):
-            g = seqs.tile([P, N], F32, name="s_rows")
-            s_rows[b] = g
-            nc.vector.tensor_copy(g[:], s_pool[b][:].indirect(lists[:, b * 32 : (b + 1) * 32]))
-            if len([j for j in range(4) if (b, j) in BY_G]) == 4:
-                return
             bank = ps_t.tile([P, PACK, P], F32, name="bank_t")
-            slots = g[:].rearrange("p (s t) -> p t s", t=PACK)
+            slots = s_rows[:, b * N : (b + 1) * N].rearrange("p (s t) -> p t s", t=PACK)
             for t in range(PACK):
                 nc.tensor.transpose(bank[:, t, :], slots[:, t, :], ident[:])
             slot_scale[b] = seqs.tile([P, PACK], F32, name="slot_scale")
@@ -199,7 +200,7 @@ def tile_attend_x_cluster_cap_kernel(tc, xq, kT, vT, vs, offs, qoffs, out):
             v_scales[b] = seqs.tile([P, DV], U8, name="scales_v", align_bytes=64)
             nc.vector.quantize_mx(out=v_codes[b][:].bitcast(FP8X4), scales=v_scales[b][:], in_=g[:])
 
-        sums, w_codes, w_scales, weights = {}, {}, {}, {}
+        sums, w_codes, w_scales, weights, capped, lows, w_rows = {}, {}, {}, {}, {}, {}, {}
 
         def score(b, j):
             bank = ps_s.tile([P, N], F32, name="bank_s")
@@ -213,29 +214,41 @@ def tile_attend_x_cluster_cap_kernel(tc, xq, kT, vT, vs, offs, qoffs, out):
                 start=True,
                 stop=True,
             )
-            th = work.tile([P, PACK, P], F32, name="th", bufs=4)
+            if j % 2 == 0:
+                capped[b, j // 2] = work.tile([P, 2, PACK, P], F32, name="th", bufs=3)
             if (b, j) in BY_G:
-                nc.scalar.activation(th[:].rearrange("q t s -> q (t s)"), bank[:], ACT.Tanh, scale=0.5)
+                nc.scalar.activation(
+                    capped[b, j // 2][:, j % 2].rearrange("q t s -> q (t s)"), bank[:], ACT.Tanh, scale=0.5
+                )
             else:
-                nc.scalar.activation(th[:], bank[:].rearrange("q (s t) -> q t s", t=PACK), ACT.Tanh, scale=0.5)
-            neg = work.tile([P, PACK, P], F32, name="neg", bufs=2)
-            low = work.tile([P, 1], F32, name="low", bufs=4)
-            nc.vector.tensor_scalar(neg[:], th[:], -2.0, None, ALU.mult, ALU.min, accum_out=low[:])
+                nc.scalar.activation(
+                    capped[b, j // 2][:, j % 2], bank[:].rearrange("q (s t) -> q t s", t=PACK), ACT.Tanh, scale=0.5
+                )
+
+        def lowest(b, h):
+            top = work.tile([P, 2], F32, name="top", bufs=3)
+            nc.vector.reduce_max(
+                top[:], capped[b, h][:].rearrange("q j t s -> q j (t s)"), axis=mybir.AxisListType.X
+            )
+            lows[b, h] = work.tile([P, 2], F32, name="low", bufs=4)
+            nc.scalar.activation(lows[b, h][:], top[:], ACT.Copy, scale=-2.0)
+
+        def exponent(b, j):
             p = work.tile([P, PACK, P], F32, name="p", bufs=4)
             if j == 0:
                 sums[b] = seqs.tile([P, NQ // P], F32, name="sums")
-            if (b, j) in BY_G:
-                nc.scalar.activation(p[:], th[:], ACT.Exp, bias=low[:], scale=2.0, accum_out=sums[b][:, j : j + 1])
-                weights[b, j] = p
-                return
-            nc.scalar.activation(p[:], th[:], ACT.Exp, bias=low[:], scale=2.0, accum_out=sums[b][:, j : j + 1])
+            i = j % 2
+            nc.scalar.activation(
+                p[:], capped[b, j // 2][:, i], ACT.Exp, bias=lows[b, j // 2][:, i : i + 1], scale=2.0,
+                accum_out=sums[b][:, j : j + 1],
+            )
             weights[b, j] = p
 
         def weigh(b, j):
             p = weights[b, j]
             if (b, j) in BY_G:
                 weighed = work.tile([P, N], BF16, name="weighed", bufs=3)
-                nc.gpsimd.tensor_tensor(weighed[:], p[:].rearrange("q t s -> q (t s)"), s_rows[b][:], ALU.mult)
+                nc.gpsimd.tensor_tensor(weighed[:], p[:].rearrange("q t s -> q (t s)"), s_rows[:, b * N : (b + 1) * N], ALU.mult)
                 turned = ps_p.tile([P, PACK, P], BF16, name="turned")
                 slots = weighed[:].rearrange("q (s t) -> q t s", t=PACK)
                 for t in range(PACK):
@@ -244,24 +257,30 @@ def tile_attend_x_cluster_cap_kernel(tc, xq, kT, vT, vs, offs, qoffs, out):
                 turned = ps_p.tile([P, PACK, P], F32, name="turned")
                 for t in range(PACK):
                     nc.tensor.transpose(turned[:, t, :], p[:, t, :], ident[:])
-            w = work.tile([P, P, PACK], BF16, name="w", align_bytes=64, bufs=4)
             if j == 0:
+                w_rows[b] = seqs.tile([P, NQ, PACK], BF16, name="w", align_bytes=64)
                 w_codes[b] = seqs.tile([P, NQ], U32, name="codes_w", align_bytes=64)
                 w_scales[b] = seqs.tile([P, NQ], U8, name="scales_w", align_bytes=64)
+            w = w_rows[b][:, j * P : (j + 1) * P, :]
             if (b, j) in BY_G:
-                nc.scalar.activation(w[:], turned[:].rearrange("s t q -> s q t"), ACT.Copy)
+                nc.scalar.activation(w, turned[:].rearrange("s t q -> s q t"), ACT.Copy)
+            elif (b, j) in BY_S:
+                for t in range(PACK):
+                    nc.scalar.activation(w[:, :, t], turned[:, t, :], ACT.Copy, scale=slot_scale[b][:, t : t + 1])
             else:
                 nc.vector.tensor_tensor(
-                    w[:],
+                    w,
                     turned[:].rearrange("s t q -> s q t"),
                     slot_scale[b][:].unsqueeze(1).to_broadcast([P, P, PACK]),
                     ALU.mult,
                 )
-            here = slice(j * P, (j + 1) * P)
+
+        def quantize_weights(b, lo, hi):
+            here = slice(lo * P, hi * P)
             nc.vector.quantize_mx(
                 out=w_codes[b][:, here].bitcast(FP8X4),
                 scales=w_scales[b][:, here],
-                in_=w[:].rearrange("s q t -> s (q t)"),
+                in_=w_rows[b][:, here, :].rearrange("s q t -> s (q t)"),
             )
 
         ready = {}
@@ -317,6 +336,8 @@ def tile_attend_x_cluster_cap_kernel(tc, xq, kT, vT, vs, offs, qoffs, out):
                 gather(d[0], d[1], d[2])
             elif kind == "qu":
                 quantize(d[0], d[1])
+            elif kind == "sg":
+                gather_scales()
             elif kind == "ss":
                 prepare_scales(d[0])
             elif kind == "vg":
@@ -325,8 +346,14 @@ def tile_attend_x_cluster_cap_kernel(tc, xq, kT, vT, vs, offs, qoffs, out):
                 prepare_values(d[0])
             elif kind == "sc":
                 score(d[0], d[1])
+            elif kind == "mx":
+                lowest(d[0], d[1])
+            elif kind == "ex":
+                exponent(d[0], d[1])
             elif kind == "we":
                 weigh(d[0], d[1])
+            elif kind == "qw":
+                quantize_weights(d[0], d[1], d[2])
             elif kind == "pr":
                 product(d[0], d[1], d[2])
             elif kind == "sp":

@@ -10,7 +10,7 @@ PACK = 4
 LOADS = "M k012 L k112 q112 q01 q10 k00 q00 v1 k102 v0 s1 s0"
 PLAN = """cak00 cak11 cak01 caq11 caq01 gaq01 caq00 gak01 gak00 vg1 cak10 gaq11 caq10 quq1 gak11 gaq00 quk1 sc10 sc11 gaq10 sc12 mx10 gak10 vv1 sc13 quk0 ex10 mx11 quq0 vg0 sc00 sc01 ex11 ex12 ex13 sg ss1 mx00 we10 we11 sc02 sc03 ss0 mx01 qw102 ex00 we12 ex03 ex01 vv0 ex02 sp104 we13 we00 pr102 qw124 we01 we03 sp004 sx102 pr124 qw034 we02 qw002 pr034 sx124 st1 sx034 qw023 pr002 sx002 pr023 sx023 st0"""
 SHARES = {"cak00": [["V",512],["S",512]], "cak11": [["S",512],["S",256],["V",256]], "cak01": [["V",512],["V",512]], "caq11": [["S",512],["S",512]], "caq01": [["S",512],["V",512]], "caq00": [["S",1024]], "cak10": [["S",512],["S",256],["V",256]], "caq10": [["S",512],["S",512]]}
-INTER = {("k", 0): "step", ("k", 1): "step", ("q", 0): "V", ("q", 1): "V"}
+INTER = {("k", 0): "G", ("k", 1): "G", ("q", 0): "V", ("q", 1): "V"}
 VS = "SV"
 BY_G = ()
 BY_S = ((0, 2),)

from contextlib import ExitStack

import concourse.mybir as mybir
from concourse.masks import make_identity

P = 128
B, N, T, D, DV, NQ = 2, 512, 2048, 512, 128, 512
SEG = T // B
PACK = 4
LOADS = "M k012 L k112 q112 q01 q10 k00 q00 v1 k102 v0 s1 s0"
PLAN = """cak00 cak11 cak01 caq11 caq01 gaq01 caq00 gak01 gak00 vg1 cak10 gaq11 caq10 quq1 gak11 gaq00 quk1 sc10 sc11 gaq10 sc12 mx10 gak10 vv1 sc13 quk0 ex10 mx11 quq0 vg0 sc00 sc01 ex11 ex12 ex13 sg ss1 mx00 we10 we11 sc02 sc03 ss0 mx01 qw102 ex00 we12 ex03 ex01 vv0 ex02 sp104 we13 we00 pr102 qw124 we01 we03 sp004 sx102 pr124 qw034 we02 qw002 pr034 sx124 st1 sx034 qw023 pr002 sx002 pr023 sx023 st0"""
SHARES = {"cak00": [["V",512],["S",512]], "cak11": [["S",512],["S",256],["V",256]], "cak01": [["V",512],["V",512]], "caq11": [["S",512],["S",512]], "caq01": [["S",512],["V",512]], "caq00": [["S",1024]], "cak10": [["S",512],["S",256],["V",256]], "caq10": [["S",512],["S",512]]}
INTER = {("k", 0): "G", ("k", 1): "G", ("q", 0): "V", ("q", 1): "V"}
VS = "SV"
BY_G = ()
BY_S = ((0, 2),)
NRAW = 7
NWORK = 4
NPS = [3,3,1,1]
ZERO = "Gk0 Gk1 Gi Vq0 Vq1 Gv Gh Gp1 Gp0"
FLOPS = 2 * B * NQ * N * (D + DV)

F32 = mybir.dt.float32
BF16 = mybir.dt.bfloat16
U32 = mybir.dt.uint32
I32 = mybir.dt.int32
U16 = mybir.dt.uint16
U8 = mybir.dt.uint8
FP8X4 = mybir.dt.float8_e4m3fn_x4
ACT = mybir.ActivationFunctionType
ALU = mybir.AluOpType


def tile_attend_x_cluster_cap_kernel(tc, xq, kT, vT, vs, offs, qoffs, out):
    nc = tc.nc
    with ExitStack() as ctx:
        keep = ctx.enter_context(tc.tile_pool(name="keep", bufs=1))
        raws = ctx.enter_context(tc.tile_pool(name="raws", bufs=1))
        seqs = ctx.enter_context(tc.tile_pool(name="seqs", bufs=2))
        work = ctx.enter_context(tc.tile_pool(name="work", bufs=NWORK))
        ps_s = ctx.enter_context(tc.psum_pool(name="ps_s", bufs=NPS[0]))
        ps_p = ctx.enter_context(tc.psum_pool(name="ps_p", bufs=NPS[1]))
        ps_y = ctx.enter_context(tc.psum_pool(name="ps_y", bufs=NPS[2]))
        ps_t = ctx.enter_context(tc.psum_pool(name="ps_t", bufs=NPS[3]))

        lists = keep.tile([P, B * N // 16], U16, name="lists")
        qlists = keep.tile([P, B * NQ // 16], U16, name="qlists")
        words, v_pool, placed = {}, {}, {}
        for b in range(B):
            wide = (b + 1) * SEG
            for name in ("k", "q"):
                for u in range(2):
                    words[name, u, b] = keep.tile([P, 2 * wide], BF16, name="words_%s%d%d" % (name, u, b))
            v_pool[b] = keep.tile([P, wide], BF16 if VS[b] == "S" else F32, name="v_pool%d" % b)
            placed[b] = keep.tile([P, wide], F32, name="placed%d" % b)
        s_pool = keep.tile([P, T], F32, name="s_pool")
        s_rows = keep.tile([P, B * N], F32, name="s_rows")
        ident = keep.tile([P, P], F32, name="ident")
        ident_h = keep.tile([P, P], BF16, name="ident_h")
        warm = keep.tile([P, 1], F32, name="warm")

        source = {"k": kT.rearrange("(p j) w -> p j w", j=PACK), "q": xq.rearrange("(p j) w -> p j w", j=PACK)}
        raw, raw_tiles = {}, {}

        def load_rows(name, u, b, lo, hi):
            if lo == 0:
                raw[name, u, b] = []
                raw_tiles[name, u, b] = raws.tile([P, 2 * SEG], F32, name="raw", bufs=NRAW)
            piece = raw_tiles[name, u, b][:, 2 * lo : 2 * hi].rearrange("p (e w) -> p e w", e=2)
            nc.sync.dma_start(
                out=piece,
                in_=source[name][:, 2 * u : 2 * u + 2, b * SEG + lo : b * SEG + hi],
            )
            raw[name, u, b].append((lo, hi, piece))

        v_raw = {}
        for step in LOADS.split():
            if step == "L":
                nc.sync.dma_start(lists[:], offs)
            elif step == "M":
                nc.sync.dma_start(qlists[:], qoffs)
            elif step[0] == "s":
                b = int(step[1])
                nc.sync.dma_start(out=s_pool[:, b * SEG : (b + 1) * SEG], in_=vs[:, b * SEG : (b + 1) * SEG])
            elif step[0] == "v":
                b = int(step[1])
                if VS[b] == "S":
                    v_raw[b] = raws.tile([P, SEG], F32, name="v_raw%d" % b)
                    nc.sync.dma_start(out=v_raw[b][:], in_=vT[:, b * SEG : (b + 1) * SEG])
                else:
                    nc.sync.dma_start(out=v_pool[b][:, b * SEG : (b + 1) * SEG], in_=vT[:, b * SEG : (b + 1) * SEG])
            else:
                parts = int(step[3]) if len(step) > 3 else 1
                for i in range(parts):
                    load_rows(step[0], int(step[1]), int(step[2]), i * SEG // parts, (i + 1) * SEG // parts)

        nc.vector.memset(warm[:], 0.0)
        nc.scalar.activation(warm[:], warm[:], ACT.Exp)
        def zero(which):
            for step in which.split():
                eng = nc.vector if step[0] == "V" else nc.gpsimd
                if step[1] in "kq":
                    eng.memset(words[step[1], int(step[2]), 1][:, 0 : 2 * SEG].bitcast(U32), 0)
                elif step[1] == "v":
                    eng.memset(v_pool[1][:, 0:SEG], 0.0)
                elif step[1] == "i":
                    make_identity(nc, ident[:])
                elif step[1] == "h":
                    make_identity(nc, ident_h[:])
                elif step[1] == "p":
                    b = int(step[2])
                    eng.memset(placed[b][:, b * SEG : (b + 1) * SEG], 0.0)

        zero(ZERO)

        def cast(name, u, b, shares):
            full = words[name, u, b][:].rearrange("p (w e) -> p w e", e=2)
            lo = 0
            for engine, width in shares:
                o = full[:, b * SEG + lo : b * SEG + lo + width, :]
                for a, z, piece in raw[name, u, b]:
                    if a <= lo < z:
                        i = piece.rearrange("p e w -> p w e")[:, lo - a : lo - a + width, :]
                if engine == "S":
                    nc.scalar.activation(o, i, ACT.Copy)
                elif engine == "G":
                    nc.gpsimd.tensor_copy(o, i)
                else:
                    nc.vector.tensor_copy(o, i)
                lo += width

        grouped, codes, scales, apart = {}, {}, {}, {}

        def gather(name, u, b):
            mode = INTER[name, b]
            if u == 0:
                grouped[name, b] = seqs.tile([P, N * PACK], BF16, name="grouped_" + name, align_bytes=64)
                if mode != "step":
                    apart[name, b] = seqs.tile([P, 2, N], U32, name="apart_" + name, bufs=1)
            window = words[name, u, b][:].bitcast(U32)
            index = lists if name == "k" else qlists
            dest = grouped[name, b][:].bitcast(U32).rearrange("p (n u) -> p n u", u=2)
            picked = window.indirect(index[:, b * 32 : (b + 1) * 32])
            if mode == "step":
                nc.vector.tensor_copy(dest[:, :, u], picked)
            else:
                nc.vector.tensor_copy(apart[name, b][:, u, :], picked)
                if u == 1:
                    src = apart[name, b][:].rearrange("p u n -> p n u")
                    if mode == "S":
                        nc.scalar.copy(dest, src)
                    elif mode == "V":
                        nc.vector.tensor_copy(
                            grouped[name, b][:].bitcast(I32).rearrange("p (n u) -> p n u", u=2),
                            apart[name, b][:].bitcast(I32).rearrange("p u n -> p n u"),
                        )
                    else:
                        nc.gpsimd.tensor_copy(dest, src)

        def quantize(name, b):
            codes[name, b] = seqs.tile([P, N], U32, name="codes_" + name, align_bytes=64)
            scales[name, b] = seqs.tile([P, N], U8, name="scales_" + name, align_bytes=64)
            nc.vector.quantize_mx(
                out=codes[name, b][:].bitcast(FP8X4), scales=scales[name, b][:], in_=grouped[name, b][:]
            )

        slot_scale, v_codes, v_scales, v_rows = {}, {}, {}, {}

        def gather_scales():
            nc.vector.tensor_copy(s_rows[:], s_pool[:].indirect(lists[:]))

        def prepare_scales(b):
            bank = ps_t.tile([P, PACK, P], F32, name="bank_t")
            slots = s_rows[:, b * N : (b + 1) * N].rearrange("p (s t) -> p t s", t=PACK)
            for t in range(PACK):
                nc.tensor.transpose(bank[:, t, :], slots[:, t, :], ident[:])
            slot_scale[b] = seqs.tile([P, PACK], F32, name="slot_scale")
            nc.scalar.activation(slot_scale[b][:], bank[:, :, 0], ACT.Copy)

        def gather_values(b):
            if VS[b] == "S":
                nc.scalar.activation(v_pool[b][:, b * SEG : (b + 1) * SEG], v_raw[b][:], ACT.Copy)
                g = seqs.tile([P, N, 2], BF16, name="v_rows_h")
                nc.scalar.activation(g[:, :, 0], v_pool[b][:].indirect(lists[:, b * 32 : (b + 1) * 32]), ACT.Copy)
                v_rows[b] = (g[:, :, 0], BF16, ident_h)
            else:
                g = seqs.tile([P, N], F32, name="v_rows")
                nc.vector.tensor_copy(g[:], v_pool[b][:].indirect(lists[:, b * 32 : (b + 1) * 32]))
                v_rows[b] = (g[:], F32, ident)

        def prepare_values(b):
            rows, kind, eye = v_rows[b]
            bank = ps_t.tile([P, PACK, P], kind, name="bank_t")
            slots = rows.rearrange("p (s t) -> p t s", t=PACK)
            for t in range(PACK):
                nc.tensor.transpose(bank[:, t, :], slots[:, t, :], eye[:])
            g = seqs.tile([P, DV * PACK], BF16, name="grouped_v", align_bytes=64)
            nc.scalar.activation(g[:].rearrange("p (e t) -> p e t", t=PACK), bank[:].rearrange("p t e -> p e t"), ACT.Copy)
            v_codes[b] = seqs.tile([P, DV], U32, name="codes_v", align_bytes=64)
            v_scales[b] = seqs.tile([P, DV], U8, name="scales_v", align_bytes=64)
            nc.vector.quantize_mx(out=v_codes[b][:].bitcast(FP8X4), scales=v_scales[b][:], in_=g[:])

        sums, w_codes, w_scales, weights, capped, lows, w_rows = {}, {}, {}, {}, {}, {}, {}

        def score(b, j):
            bank = ps_s.tile([P, N], F32, name="bank_s")
            cols = slice(j * P, (j + 1) * P)
            nc.tensor.matmul_mx(
                out=bank[:],
                lhsT=codes["q", b][:, cols].bitcast(FP8X4),
                lhsT_scale=scales["q", b][:, cols],
                rhs=codes["k", b][:].bitcast(FP8X4),
                rhs_scale=scales["k", b][:],
                start=True,
                stop=True,
            )
            if j % 2 == 0:
                capped[b, j // 2] = work.tile([P, 2, PACK, P], F32, name="th", bufs=3)
            if (b, j) in BY_G:
                nc.scalar.activation(
                    capped[b, j // 2][:, j % 2].rearrange("q t s -> q (t s)"), bank[:], ACT.Tanh, scale=0.5
                )
            else:
                nc.scalar.activation(
                    capped[b, j // 2][:, j % 2], bank[:].rearrange("q (s t) -> q t s", t=PACK), ACT.Tanh, scale=0.5
                )

        def lowest(b, h):
            top = work.tile([P, 2], F32, name="top", bufs=3)
            nc.vector.reduce_max(
                top[:], capped[b, h][:].rearrange("q j t s -> q j (t s)"), axis=mybir.AxisListType.X
            )
            lows[b, h] = work.tile([P, 2], F32, name="low", bufs=4)
            nc.scalar.activation(lows[b, h][:], top[:], ACT.Copy, scale=-2.0)

        def exponent(b, j):
            p = work.tile([P, PACK, P], F32, name="p", bufs=4)
            if j == 0:
                sums[b] = seqs.tile([P, NQ // P], F32, name="sums")
            i = j % 2
            nc.scalar.activation(
                p[:], capped[b, j // 2][:, i], ACT.Exp, bias=lows[b, j // 2][:, i : i + 1], scale=2.0,
                accum_out=sums[b][:, j : j + 1],
            )
            weights[b, j] = p

        def weigh(b, j):
            p = weights[b, j]
            if (b, j) in BY_G:
                weighed = work.tile([P, N], BF16, name="weighed", bufs=3)
                nc.gpsimd.tensor_tensor(weighed[:], p[:].rearrange("q t s -> q (t s)"), s_rows[:, b * N : (b + 1) * N], ALU.mult)
                turned = ps_p.tile([P, PACK, P], BF16, name="turned")
                slots = weighed[:].rearrange("q (s t) -> q t s", t=PACK)
                for t in range(PACK):
                    nc.tensor.transpose(turned[:, t, :], slots[:, t, :], ident_h[:])
            else:
                turned = ps_p.tile([P, PACK, P], F32, name="turned")
                for t in range(PACK):
                    nc.tensor.transpose(turned[:, t, :], p[:, t, :], ident[:])
            if j == 0:
                w_rows[b] = seqs.tile([P, NQ, PACK], BF16, name="w", align_bytes=64)
                w_codes[b] = seqs.tile([P, NQ], U32, name="codes_w", align_bytes=64)
                w_scales[b] = seqs.tile([P, NQ], U8, name="scales_w", align_bytes=64)
            w = w_rows[b][:, j * P : (j + 1) * P, :]
            if (b, j) in BY_G:
                nc.scalar.activation(w, turned[:].rearrange("s t q -> s q t"), ACT.Copy)
            elif (b, j) in BY_S:
                for t in range(PACK):
                    nc.scalar.activation(w[:, :, t], turned[:, t, :], ACT.Copy, scale=slot_scale[b][:, t : t + 1])
            else:
                nc.vector.tensor_tensor(
                    w,
                    turned[:].rearrange("s t q -> s q t"),
                    slot_scale[b][:].unsqueeze(1).to_broadcast([P, P, PACK]),
                    ALU.mult,
                )

        def quantize_weights(b, lo, hi):
            here = slice(lo * P, hi * P)
            nc.vector.quantize_mx(
                out=w_codes[b][:, here].bitcast(FP8X4),
                scales=w_scales[b][:, here],
                in_=w_rows[b][:, here, :].rearrange("s q t -> s (q t)"),
            )

        ready = {}

        def product(b, lo, hi):
            width = (hi - lo) * P
            bank = ps_y.tile([P, width], F32, name="bank_y")
            nc.tensor.matmul_mx(
                out=bank[:],
                lhsT=v_codes[b][:].bitcast(FP8X4),
                lhsT_scale=v_scales[b][:],
                rhs=w_codes[b][:, lo * P : hi * P].bitcast(FP8X4),
                rhs_scale=w_scales[b][:, lo * P : hi * P],
                start=True,
                stop=True,
            )
            y = work.tile([P, width], F32, name="y", bufs=4)
            nc.scalar.activation(y[:], bank[:], ACT.Copy)
            ready[b, lo] = y

        factors = {}

        def spread(b, lo, hi):
            inv = work.tile([P, hi - lo], F32, name="inv", bufs=2)
            nc.vector.reciprocal(inv[:], sums[b][:, lo:hi])
            bank = ps_t.tile([P, hi - lo, P], F32, name="bank_t")
            for i in range(hi - lo):
                nc.tensor.transpose(bank[:, i, :], inv[:, i : i + 1].to_broadcast([P, P]), ident[:])
            factor = work.tile([P, (hi - lo) * P], F32, name="factor", bufs=2)
            nc.scalar.activation(factor[:], bank[:].rearrange("p i q -> p (i q)"), ACT.Copy)
            for i in range(hi - lo):
                factors[b, lo + i] = (factor, i)

        def scatter(b, lo, hi):
            factor, i = factors[b, lo]
            first = b * 32 + 8 * lo
            nc.vector.tensor_tensor(
                placed[b][:].indirect(qlists[:, first : first + 8 * (hi - lo)]),
                ready[b, lo][:],
                factor[:, i * P : (i + hi - lo) * P],
                ALU.mult,
            )

        def store(b):
            nc.sync.dma_start(out=out[:, b * SEG : (b + 1) * SEG], in_=placed[b][:, b * SEG : (b + 1) * SEG])

        for step in PLAN.split():
            kind, rest = step[:2], step[2:]
            d = [c if c in "kq" else int(c) for c in rest]
            if kind == "ca":
                cast(d[0], d[1], d[2], SHARES[step])
            elif kind == "ga":
                gather(d[0], d[1], d[2])
            elif kind == "qu":
                quantize(d[0], d[1])
            elif kind == "sg":
                gather_scales()
            elif kind == "ss":
                prepare_scales(d[0])
            elif kind == "vg":
                gather_values(d[0])
            elif kind == "vv":
                prepare_values(d[0])
            elif kind == "sc":
                score(d[0], d[1])
            elif kind == "mx":
                lowest(d[0], d[1])
            elif kind == "ex":
                exponent(d[0], d[1])
            elif kind == "we":
                weigh(d[0], d[1])
            elif kind == "qw":
                quantize_weights(d[0], d[1], d[2])
            elif kind == "pr":
                product(d[0], d[1], d[2])
            elif kind == "sp":
                spread(d[0], d[1], d[2])
            elif kind == "sx":
                scatter(d[0], d[1], d[2])
            elif kind == "st":
                store(d[0])
            else:
                assert False
